import numpy as np
import ml_dtypes

BF16 = ml_dtypes.bfloat16


def bf(x):
    return np.asarray(x, np.float32).astype(BF16)


def f32(x):
    return np.asarray(x, np.float32)


def f64(x):
    return np.asarray(x).astype(np.float64)


def striped(idx):
    return np.tile(idx.reshape(-1, 16).T, (8, 1))


S, K, M, N, D, V = 2048, 256, 512, 1024, 8, 128


def gelu_tanh(v):
    return 0.5 * v * (1.0 + np.tanh(np.sqrt(2.0 / np.pi) * (v + 0.044715 * v**3)))


def setup_inputs():
    return {"table": bf(np.random.standard_normal((K, S))), "w": bf(np.random.standard_normal((K, M)) / np.sqrt(K)), "b": f32(0.5 * np.random.standard_normal((M, 1))), "offs": striped(np.random.permutation(np.tile(np.arange(S), 2))[:N])}


def reference(table, w, b, offs):
    idx = offs[:16].T.reshape(-1)
    x = f64(table)[:, idx]
    y = f64(w).T @ x
    z = gelu_tanh(y + f64(b))
    return z.reshape(M, V, D).max(axis=2)

@@ -1,0 +1,69 @@
+import concourse.mybir as mybir
+
+BF16, F32, U16 = mybir.dt.bfloat16, mybir.dt.float32, mybir.dt.uint16
+
+P = 128
+K, S = 256, 2048
+M = 512
+N = 1024
+PIECE = 512
+NEIGHBOURS = 8
+
+K_BLOCKS = K // P
+M_BLOCKS = M // P
+PIECES = N // PIECE
+POOLED = PIECE // NEIGHBOURS
+
+FLOPS = 2 * K * M * N
+
+
+def tile_gather_matmul_kernel(tc, table, w, b, offs, out):
+    nc = tc.nc
+    with (
+        tc.tile_pool(name="held", bufs=1) as held,
+        tc.tile_pool(name="work", bufs=3) as work,
+        tc.psum_pool(name="psum", bufs=1) as psum,
+    ):
+        offsets = held.tile([P, N // 16], U16, name="offsets")
+        nc.sync.dma_start(offsets[:], offs)
+        weights = held.tile([P, K_BLOCKS, M], BF16, name="weights")
+        nc.scalar.dma_start(weights[:], w.rearrange("(k p) m -> p k m", p=P))
+        windows = [held.tile([P, S], BF16, name=f"window{k}") for k in range(K_BLOCKS)]
+        nc.sync.dma_start(windows[0][:], table[0:P, :])
+        nc.scalar.dma_start(windows[1][:], table[P : 2 * P, :])
+        bias = held.tile([P, M_BLOCKS], F32, name="bias")
+        with nc.allow_non_contiguous_dma(reason="one float32 to a partition and block: 512 small pieces"):
+            nc.gpsimd.dma_start(bias[:], b.rearrange("(a p) o -> p (a o)", p=P))
+
+        banks = {
+            (a, q): psum.tile([P, PIECE], F32, name=f"bank{a}{q}")
+            for a in range(M_BLOCKS)
+            for q in range(PIECES)
+        }
+
+        for k in range(K_BLOCKS):
+            for a in range(M_BLOCKS):
+                for q in range(PIECES):
+                    picked = windows[k][:].indirect(offsets[:, q * (PIECE // 16) : (q + 1) * (PIECE // 16)])
+                    nc.tensor.matmul(
+                        banks[a, q][:],
+                        weights[:, k, a * P : (a + 1) * P],
+                        picked,
+                        start=(k == 0),
+                        stop=(k == K_BLOCKS - 1),
+                    )
+
+        for a in range(M_BLOCKS):
+            pooled = work.tile([P, PIECES * POOLED], F32, name="pooled")
+            for q in range(PIECES):
+                z = work.tile([P, PIECE], F32, name="z")
+                nc.scalar.activation(
+                    z[:], banks[a, q][:], mybir.ActivationFunctionType.Gelu_apprx_tanh, bias=bias[:, a : a + 1]
+                )
+                nc.vector.tensor_reduce(
+                    pooled[:, q * POOLED : (q + 1) * POOLED],
+                    z[:].rearrange("p (v t) -> p v t", t=NEIGHBOURS),
+                    axis=mybir.AxisListType.X,
+                    op=mybir.AluOpType.max,
+                )
+            nc.sync.dma_start(out[a * P : (a + 1) * P, :], pooled[:])

@@ -26,11 +26,14 @@ def tile_gather_matmul_kernel(tc, table, w, b, offs, out):
     ):
         offsets = held.tile([P, N // 16], U16, name="offsets")
         nc.sync.dma_start(offsets[:], offs)
-        weights = held.tile([P, K_BLOCKS, M], BF16, name="weights")
-        nc.scalar.dma_start(weights[:], w.rearrange("(k p) m -> p k m", p=P))
         windows = [held.tile([P, S], BF16, name=f"window{k}") for k in range(K_BLOCKS)]
-        nc.sync.dma_start(windows[0][:], table[0:P, :])
-        nc.scalar.dma_start(windows[1][:], table[P : 2 * P, :])
+        weights = [held.tile([P, M], BF16, name=f"weights{k}") for k in range(K_BLOCKS)]
+        for k in range(K_BLOCKS):
+            rows = slice(k * P, (k + 1) * P)
+            for tile_k, source, columns in ((weights[k], w, M), (windows[k], table, S)):
+                half = columns // 2
+                nc.sync.dma_start(tile_k[:, 0:half], source[rows, 0:half])
+                nc.scalar.dma_start(tile_k[:, half:columns], source[rows, half:columns])
         bias = held.tile([P, M_BLOCKS], F32, name="bias")
         with nc.allow_non_contiguous_dma(reason="one float32 to a partition and block: 512 small pieces"):
             nc.gpsimd.dma_start(bias[:], b.rearrange("(a p) o -> p (a o)", p=P))
@@ -47,7 +50,7 @@ def tile_gather_matmul_kernel(tc, table, w, b, offs, out):
                     picked = windows[k][:].indirect(offsets[:, q * (PIECE // 16) : (q + 1) * (PIECE // 16)])
                     nc.tensor.matmul(
                         banks[a, q][:],
-                        weights[:, k, a * P : (a + 1) * P],
+                        weights[k][:, a * P : (a + 1) * P],
                         picked,
                         start=(k == 0),
                         stop=(k == K_BLOCKS - 1),

@@ -14,6 +14,8 @@ M_BLOCKS = M // P
 PIECES = N // PIECE
 POOLED = PIECE // NEIGHBOURS
 
+WARM_UP = 8
+
 FLOPS = 2 * K * M * N
 
 
@@ -43,6 +45,11 @@ def tile_gather_matmul_kernel(tc, table, w, b, offs, out):
             for a in range(M_BLOCKS)
             for q in range(PIECES)
         }
+
+        zeros = held.tile([P, PIECE], BF16, name="zeros")
+        nc.vector.memset(zeros[:], 0.0)
+        for warm in range(WARM_UP):
+            nc.tensor.matmul(banks[0, 0][:], zeros[:, 0:P], zeros[:], start=True, stop=True)
 
         for k in range(K_BLOCKS):
             for a in range(M_BLOCKS):

@@ -14,8 +14,6 @@ M_BLOCKS = M // P
 PIECES = N // PIECE
 POOLED = PIECE // NEIGHBOURS
 
-WARM_UP = 8
-
 FLOPS = 2 * K * M * N
 
 
@@ -38,18 +36,18 @@ def tile_gather_matmul_kernel(tc, table, w, b, offs, out):
                 nc.scalar.dma_start(tile_k[:, half:columns], source[rows, half:columns])
         bias = held.tile([P, M_BLOCKS], F32, name="bias")
         with nc.allow_non_contiguous_dma(reason="one float32 to a partition and block: 512 small pieces"):
-            nc.gpsimd.dma_start(bias[:], b.rearrange("(a p) o -> p (a o)", p=P))
+            nc.sync.dma_start(bias[:], b.rearrange("(a p) o -> p (a o)", p=P))
+
+        primer = held.tile([P, 1], F32, name="primer")
+        nc.vector.memset(primer[:], 0.0)
+        primed = held.tile([P, 1], F32, name="primed")
+        nc.scalar.activation(primed[:], primer[:], mybir.ActivationFunctionType.Gelu_apprx_tanh)
 
         banks = {
             (a, q): psum.tile([P, PIECE], F32, name=f"bank{a}{q}")
             for a in range(M_BLOCKS)
             for q in range(PIECES)
         }
-
-        zeros = held.tile([P, PIECE], BF16, name="zeros")
-        nc.vector.memset(zeros[:], 0.0)
-        for warm in range(WARM_UP):
-            nc.tensor.matmul(banks[0, 0][:], zeros[:, 0:P], zeros[:], start=True, stop=True)
 
         for k in range(K_BLOCKS):
             for a in range(M_BLOCKS):

@@ -14,6 +14,9 @@ M_BLOCKS = M // P
 PIECES = N // PIECE
 POOLED = PIECE // NEIGHBOURS
 
+assert K_BLOCKS == 2
+LEAD = M_BLOCKS * PIECES // 2
+
 FLOPS = 2 * K * M * N
 
 
@@ -49,29 +52,35 @@ def tile_gather_matmul_kernel(tc, table, w, b, offs, out):
             for q in range(PIECES)
         }
 
-        for k in range(K_BLOCKS):
-            for a in range(M_BLOCKS):
-                for q in range(PIECES):
-                    picked = windows[k][:].indirect(offsets[:, q * (PIECE // 16) : (q + 1) * (PIECE // 16)])
-                    nc.tensor.matmul(
-                        banks[a, q][:],
-                        weights[k][:, a * P : (a + 1) * P],
-                        picked,
-                        start=(k == 0),
-                        stop=(k == K_BLOCKS - 1),
-                    )
+        def gathered_matmul(k, a, q):
+            picked = windows[k][:].indirect(offsets[:, q * (PIECE // 16) : (q + 1) * (PIECE // 16)])
+            nc.tensor.matmul(
+                banks[a, q][:],
+                weights[k][:, a * P : (a + 1) * P],
+                picked,
+                start=(k == 0),
+                stop=(k == K_BLOCKS - 1),
+            )
 
-        for a in range(M_BLOCKS):
-            pooled = work.tile([P, PIECES * POOLED], F32, name="pooled")
-            for q in range(PIECES):
+        output_tiles = [(a, q) for a in range(M_BLOCKS) for q in range(PIECES)]
+        pooled_blocks = {}
+        for step in range(len(output_tiles) + LEAD):
+            if step >= LEAD:
+                a, q = output_tiles[step - LEAD]
+                gathered_matmul(1, a, q)
                 z = work.tile([P, PIECE], F32, name="z")
                 nc.scalar.activation(
                     z[:], banks[a, q][:], mybir.ActivationFunctionType.Gelu_apprx_tanh, bias=bias[:, a : a + 1]
                 )
+                if q == 0:
+                    pooled_blocks[a] = work.tile([P, PIECES * POOLED], F32, name="pooled")
                 nc.vector.tensor_reduce(
-                    pooled[:, q * POOLED : (q + 1) * POOLED],
+                    pooled_blocks[a][:, q * POOLED : (q + 1) * POOLED],
                     z[:].rearrange("p (v t) -> p v t", t=NEIGHBOURS),
                     axis=mybir.AxisListType.X,
                     op=mybir.AluOpType.max,
                 )
-            nc.sync.dma_start(out[a * P : (a + 1) * P, :], pooled[:])
+                if q == PIECES - 1:
+                    nc.sync.dma_start(out[a * P : (a + 1) * P, :], pooled_blocks[a][:])
+            if step < len(output_tiles):
+                gathered_matmul(0, *output_tiles[step])

@@ -15,7 +15,7 @@ PIECES = N // PIECE
 POOLED = PIECE // NEIGHBOURS
 
 assert K_BLOCKS == 2
-LEAD = M_BLOCKS * PIECES // 2
+LEAD = 3
 
 FLOPS = 2 * K * M * N
 
@@ -62,25 +62,30 @@ def tile_gather_matmul_kernel(tc, table, w, b, offs, out):
                 stop=(k == K_BLOCKS - 1),
             )
 
-        output_tiles = [(a, q) for a in range(M_BLOCKS) for q in range(PIECES)]
         pooled_blocks = {}
-        for step in range(len(output_tiles) + LEAD):
-            if step >= LEAD:
-                a, q = output_tiles[step - LEAD]
-                gathered_matmul(1, a, q)
-                z = work.tile([P, PIECE], F32, name="z")
-                nc.scalar.activation(
-                    z[:], banks[a, q][:], mybir.ActivationFunctionType.Gelu_apprx_tanh, bias=bias[:, a : a + 1]
-                )
-                if q == 0:
-                    pooled_blocks[a] = work.tile([P, PIECES * POOLED], F32, name="pooled")
-                nc.vector.tensor_reduce(
-                    pooled_blocks[a][:, q * POOLED : (q + 1) * POOLED],
-                    z[:].rearrange("p (v t) -> p v t", t=NEIGHBOURS),
-                    axis=mybir.AxisListType.X,
-                    op=mybir.AluOpType.max,
-                )
-                if q == PIECES - 1:
-                    nc.sync.dma_start(out[a * P : (a + 1) * P, :], pooled_blocks[a][:])
-            if step < len(output_tiles):
-                gathered_matmul(0, *output_tiles[step])
+
+        def close_and_pool(a, q):
+            gathered_matmul(1, a, q)
+            z = work.tile([P, PIECE], F32, name="z")
+            nc.scalar.activation(
+                z[:], banks[a, q][:], mybir.ActivationFunctionType.Gelu_apprx_tanh, bias=bias[:, a : a + 1]
+            )
+            if q == 0:
+                pooled_blocks[a] = work.tile([P, PIECES * POOLED], F32, name="pooled")
+            nc.vector.tensor_reduce(
+                pooled_blocks[a][:, q * POOLED : (q + 1) * POOLED],
+                z[:].rearrange("p (v t) -> p v t", t=NEIGHBOURS),
+                axis=mybir.AxisListType.X,
+                op=mybir.AluOpType.max,
+            )
+            if q == PIECES - 1:
+                nc.sync.dma_start(out[a * P : (a + 1) * P, :], pooled_blocks[a][:])
+
+        output_tiles = [(a, q) for a in range(M_BLOCKS) for q in range(PIECES)]
+        for a, q in output_tiles[:LEAD]:
+            gathered_matmul(0, a, q)
+        for a, q in output_tiles[:LEAD]:
+            close_and_pool(a, q)
+        for a, q in output_tiles[LEAD:]:
+            gathered_matmul(0, a, q)
+            close_and_pool(a, q)

@@ -64,20 +64,26 @@ def tile_gather_matmul_kernel(tc, table, w, b, offs, out):
 
         pooled_blocks = {}
 
-        def close_and_pool(a, q):
+        def close_and_pool(a, q, cuts):
             gathered_matmul(1, a, q)
-            z = work.tile([P, PIECE], F32, name="z")
-            nc.scalar.activation(
-                z[:], banks[a, q][:], mybir.ActivationFunctionType.Gelu_apprx_tanh, bias=bias[:, a : a + 1]
-            )
             if q == 0:
                 pooled_blocks[a] = work.tile([P, PIECES * POOLED], F32, name="pooled")
-            nc.vector.tensor_reduce(
-                pooled_blocks[a][:, q * POOLED : (q + 1) * POOLED],
-                z[:].rearrange("p (v t) -> p v t", t=NEIGHBOURS),
-                axis=mybir.AxisListType.X,
-                op=mybir.AluOpType.max,
-            )
+            run = PIECE // cuts
+            for c in range(cuts):
+                z = work.tile([P, run], F32, name="z")
+                nc.scalar.activation(
+                    z[:],
+                    banks[a, q][:, c * run : (c + 1) * run],
+                    mybir.ActivationFunctionType.Gelu_apprx_tanh,
+                    bias=bias[:, a : a + 1],
+                )
+                first = q * POOLED + c * (run // NEIGHBOURS)
+                nc.vector.tensor_reduce(
+                    pooled_blocks[a][:, first : first + run // NEIGHBOURS],
+                    z[:].rearrange("p (v t) -> p v t", t=NEIGHBOURS),
+                    axis=mybir.AxisListType.X,
+                    op=mybir.AluOpType.max,
+                )
             if q == PIECES - 1:
                 nc.sync.dma_start(out[a * P : (a + 1) * P, :], pooled_blocks[a][:])
 
@@ -85,7 +91,7 @@ def tile_gather_matmul_kernel(tc, table, w, b, offs, out):
         for a, q in output_tiles[:LEAD]:
             gathered_matmul(0, a, q)
         for a, q in output_tiles[:LEAD]:
-            close_and_pool(a, q)
+            close_and_pool(a, q, cuts=1)
         for a, q in output_tiles[LEAD:]:
             gathered_matmul(0, a, q)
-            close_and_pool(a, q)
+            close_and_pool(a, q, cuts=2 if (a, q) == output_tiles[-1] else 1)

@@ -31,12 +31,14 @@ def tile_gather_matmul_kernel(tc, table, w, b, offs, out):
         nc.sync.dma_start(offsets[:], offs)
         windows = [held.tile([P, S], BF16, name=f"window{k}") for k in range(K_BLOCKS)]
         weights = [held.tile([P, M], BF16, name=f"weights{k}") for k in range(K_BLOCKS)]
-        for k in range(K_BLOCKS):
-            rows = slice(k * P, (k + 1) * P)
-            for tile_k, source, columns in ((weights[k], w, M), (windows[k], table, S)):
-                half = columns // 2
-                nc.sync.dma_start(tile_k[:, 0:half], source[rows, 0:half])
-                nc.scalar.dma_start(tile_k[:, half:columns], source[rows, half:columns])
+        half = S // 2
+        nc.scalar.dma_start(weights[0][:, 0:P], w[0:P, 0:P])
+        nc.sync.dma_start(windows[0][:, 0:half], table[0:P, 0:half])
+        nc.scalar.dma_start(windows[0][:, half:S], table[0:P, half:S])
+        nc.sync.dma_start(weights[0][:, P:M], w[0:P, P:M])
+        nc.scalar.dma_start(weights[1][:], w[P : 2 * P, :])
+        nc.sync.dma_start(windows[1][:, 0:half], table[P : 2 * P, 0:half])
+        nc.scalar.dma_start(windows[1][:, half:S], table[P : 2 * P, half:S])
         bias = held.tile([P, M_BLOCKS], F32, name="bias")
         with nc.allow_non_contiguous_dma(reason="one float32 to a partition and block: 512 small pieces"):
             nc.sync.dma_start(bias[:], b.rearrange("(a p) o -> p (a o)", p=P))

@@ -15,7 +15,7 @@ PIECES = N // PIECE
 POOLED = PIECE // NEIGHBOURS
 
 assert K_BLOCKS == 2
-LEAD = 3
+LEAD = 6
 
 FLOPS = 2 * K * M * N
 
@@ -25,7 +25,7 @@ def tile_gather_matmul_kernel(tc, table, w, b, offs, out):
     with (
         tc.tile_pool(name="held", bufs=1) as held,
         tc.tile_pool(name="work", bufs=3) as work,
-        tc.psum_pool(name="psum", bufs=1) as psum,
+        tc.psum_pool(name="psum", bufs=LEAD) as psum,
     ):
         offsets = held.tile([P, N // 16], U16, name="offsets")
         nc.sync.dma_start(offsets[:], offs)
@@ -48,11 +48,7 @@ def tile_gather_matmul_kernel(tc, table, w, b, offs, out):
         primed = held.tile([P, 1], F32, name="primed")
         nc.scalar.activation(primed[:], primer[:], mybir.ActivationFunctionType.Gelu_apprx_tanh)
 
-        banks = {
-            (a, q): psum.tile([P, PIECE], F32, name=f"bank{a}{q}")
-            for a in range(M_BLOCKS)
-            for q in range(PIECES)
-        }
+        banks = {}
 
         def gathered_matmul(k, a, q):
             picked = windows[k][:].indirect(offsets[:, q * (PIECE // 16) : (q + 1) * (PIECE // 16)])
@@ -63,6 +59,10 @@ def tile_gather_matmul_kernel(tc, table, w, b, offs, out):
                 start=(k == 0),
                 stop=(k == K_BLOCKS - 1),
             )
+
+        def open_bank(a, q):
+            banks[a, q] = psum.tile([P, PIECE], F32, name="bank")
+            gathered_matmul(0, a, q)
 
         pooled_blocks = {}
 
@@ -91,9 +91,9 @@ def tile_gather_matmul_kernel(tc, table, w, b, offs, out):
 
         output_tiles = [(a, q) for a in range(M_BLOCKS) for q in range(PIECES)]
         for a, q in output_tiles[:LEAD]:
-            gathered_matmul(0, a, q)
+            open_bank(a, q)
         for a, q in output_tiles[:LEAD]:
             close_and_pool(a, q, cuts=1)
         for a, q in output_tiles[LEAD:]:
-            gathered_matmul(0, a, q)
+            open_bank(a, q)
             close_and_pool(a, q, cuts=2 if (a, q) == output_tiles[-1] else 1)

@@ -16,6 +16,7 @@ POOLED = PIECE // NEIGHBOURS
 
 assert K_BLOCKS == 2
 LEAD = 6
+LAST_CUTS = 4
 
 FLOPS = 2 * K * M * N
 
@@ -24,7 +25,7 @@ def tile_gather_matmul_kernel(tc, table, w, b, offs, out):
     nc = tc.nc
     with (
         tc.tile_pool(name="held", bufs=1) as held,
-        tc.tile_pool(name="work", bufs=3) as work,
+        tc.tile_pool(name="work", bufs=LAST_CUTS + 2) as work,
         tc.psum_pool(name="psum", bufs=LEAD) as psum,
     ):
         offsets = held.tile([P, N // 16], U16, name="offsets")
@@ -96,4 +97,4 @@ def tile_gather_matmul_kernel(tc, table, w, b, offs, out):
             close_and_pool(a, q, cuts=1)
         for a, q in output_tiles[LEAD:]:
             open_bank(a, q)
-            close_and_pool(a, q, cuts=2 if (a, q) == output_tiles[-1] else 1)
+            close_and_pool(a, q, cuts=LAST_CUTS if (a, q) == output_tiles[-1] else 1)

@@ -97,4 +97,4 @@ def tile_gather_matmul_kernel(tc, table, w, b, offs, out):
             close_and_pool(a, q, cuts=1)
         for a, q in output_tiles[LEAD:]:
             open_bank(a, q)
-            close_and_pool(a, q, cuts=LAST_CUTS if (a, q) == output_tiles[-1] else 1)
+            close_and_pool(a, q, cuts=LAST_CUTS)

@@ -33,9 +33,9 @@ def tile_gather_matmul_kernel(tc, table, w, b, offs, out):
         windows = [held.tile([P, S], BF16, name=f"window{k}") for k in range(K_BLOCKS)]
         weights = [held.tile([P, M], BF16, name=f"weights{k}") for k in range(K_BLOCKS)]
         half = S // 2
-        nc.scalar.dma_start(weights[0][:, 0:P], w[0:P, 0:P])
-        nc.sync.dma_start(windows[0][:, 0:half], table[0:P, 0:half])
         nc.scalar.dma_start(windows[0][:, half:S], table[0:P, half:S])
+        nc.sync.dma_start(windows[0][:, 0:half], table[0:P, 0:half])
+        nc.scalar.dma_start(weights[0][:, 0:P], w[0:P, 0:P])
         nc.sync.dma_start(weights[0][:, P:M], w[0:P, P:M])
         nc.scalar.dma_start(weights[1][:], w[P : 2 * P, :])
         nc.sync.dma_start(windows[1][:, 0:half], table[P : 2 * P, 0:half])

@@ -33,8 +33,12 @@ def tile_gather_matmul_kernel(tc, table, w, b, offs, out):
         windows = [held.tile([P, S], BF16, name=f"window{k}") for k in range(K_BLOCKS)]
         weights = [held.tile([P, M], BF16, name=f"weights{k}") for k in range(K_BLOCKS)]
         half = S // 2
-        nc.scalar.dma_start(windows[0][:, half:S], table[0:P, half:S])
-        nc.sync.dma_start(windows[0][:, 0:half], table[0:P, 0:half])
+        quarter = S // 4
+        for c in (0, 1):
+            right = half + c * quarter
+            left = c * quarter
+            nc.scalar.dma_start(windows[0][:, right : right + quarter], table[0:P, right : right + quarter])
+            nc.sync.dma_start(windows[0][:, left : left + quarter], table[0:P, left : left + quarter])
         nc.scalar.dma_start(weights[0][:, 0:P], w[0:P, 0:P])
         nc.sync.dma_start(weights[0][:, P:M], w[0:P, P:M])
         nc.scalar.dma_start(weights[1][:], w[P : 2 * P, :])

@@ -48,10 +48,8 @@ def tile_gather_matmul_kernel(tc, table, w, b, offs, out):
         with nc.allow_non_contiguous_dma(reason="one float32 to a partition and block: 512 small pieces"):
             nc.sync.dma_start(bias[:], b.rearrange("(a p) o -> p (a o)", p=P))
 
-        primer = held.tile([P, 1], F32, name="primer")
-        nc.vector.memset(primer[:], 0.0)
         primed = held.tile([P, 1], F32, name="primed")
-        nc.scalar.activation(primed[:], primer[:], mybir.ActivationFunctionType.Gelu_apprx_tanh)
+        nc.scalar.activation(primed[:], weights[0][:, 0:1], mybir.ActivationFunctionType.Gelu_apprx_tanh)
 
         banks = {}
 

@@ -33,15 +33,13 @@ def tile_gather_matmul_kernel(tc, table, w, b, offs, out):
         windows = [held.tile([P, S], BF16, name=f"window{k}") for k in range(K_BLOCKS)]
         weights = [held.tile([P, M], BF16, name=f"weights{k}") for k in range(K_BLOCKS)]
         half = S // 2
-        quarter = S // 4
-        for c in (0, 1):
-            right = half + c * quarter
-            left = c * quarter
-            nc.scalar.dma_start(windows[0][:, right : right + quarter], table[0:P, right : right + quarter])
-            nc.sync.dma_start(windows[0][:, left : left + quarter], table[0:P, left : left + quarter])
+        nc.scalar.dma_start(windows[0][:, half:S], table[0:P, half:S])
+        nc.sync.dma_start(windows[0][:, 0:half], table[0:P, 0:half])
         nc.scalar.dma_start(weights[0][:, 0:P], w[0:P, 0:P])
-        nc.sync.dma_start(weights[0][:, P:M], w[0:P, P:M])
-        nc.scalar.dma_start(weights[1][:], w[P : 2 * P, :])
+        nc.sync.dma_start(weights[0][:, P : 2 * P], w[0:P, P : 2 * P])
+        nc.sync.dma_start(weights[0][:, 2 * P : M], w[0:P, 2 * P : M])
+        nc.scalar.dma_start(weights[1][:, 0 : M // 2], w[P : 2 * P, 0 : M // 2])
+        nc.scalar.dma_start(weights[1][:, M // 2 : M], w[P : 2 * P, M // 2 : M])
         nc.sync.dma_start(windows[1][:, 0:half], table[P : 2 * P, 0:half])
         nc.scalar.dma_start(windows[1][:, half:S], table[P : 2 * P, half:S])
         bias = held.tile([P, M_BLOCKS], F32, name="bias")

import concourse.mybir as mybir

BF16, F32, U16 = mybir.dt.bfloat16, mybir.dt.float32, mybir.dt.uint16

P = 128
K, S = 256, 2048
M = 512
N = 1024
PIECE = 512
NEIGHBOURS = 8

K_BLOCKS = K // P
M_BLOCKS = M // P
PIECES = N // PIECE
POOLED = PIECE // NEIGHBOURS

assert K_BLOCKS == 2
LEAD = 6
LAST_CUTS = 4

FLOPS = 2 * K * M * N


def tile_gather_matmul_kernel(tc, table, w, b, offs, out):
    nc = tc.nc
    with (
        tc.tile_pool(name="held", bufs=1) as held,
        tc.tile_pool(name="work", bufs=LAST_CUTS + 2) as work,
        tc.psum_pool(name="psum", bufs=LEAD) as psum,
    ):
        offsets = held.tile([P, N // 16], U16, name="offsets")
        nc.sync.dma_start(offsets[:], offs)
        windows = [held.tile([P, S], BF16, name=f"window{k}") for k in range(K_BLOCKS)]
        weights = [held.tile([P, M], BF16, name=f"weights{k}") for k in range(K_BLOCKS)]
        half = S // 2
        nc.scalar.dma_start(windows[0][:, half:S], table[0:P, half:S])
        nc.sync.dma_start(windows[0][:, 0:half], table[0:P, 0:half])
        nc.scalar.dma_start(weights[0][:, 0:P], w[0:P, 0:P])
        nc.sync.dma_start(weights[0][:, P : 2 * P], w[0:P, P : 2 * P])
        nc.sync.dma_start(weights[0][:, 2 * P : M], w[0:P, 2 * P : M])
        nc.scalar.dma_start(weights[1][:, 0 : M // 2], w[P : 2 * P, 0 : M // 2])
        nc.scalar.dma_start(weights[1][:, M // 2 : M], w[P : 2 * P, M // 2 : M])
        nc.sync.dma_start(windows[1][:, 0:half], table[P : 2 * P, 0:half])
        nc.scalar.dma_start(windows[1][:, half:S], table[P : 2 * P, half:S])
        bias = held.tile([P, M_BLOCKS], F32, name="bias")
        with nc.allow_non_contiguous_dma(reason="one float32 to a partition and block: 512 small pieces"):
            nc.sync.dma_start(bias[:], b.rearrange("(a p) o -> p (a o)", p=P))

        primed = held.tile([P, 1], F32, name="primed")
        nc.scalar.activation(primed[:], weights[0][:, 0:1], mybir.ActivationFunctionType.Gelu_apprx_tanh)

        banks = {}

        def gathered_matmul(k, a, q):
            picked = windows[k][:].indirect(offsets[:, q * (PIECE // 16) : (q + 1) * (PIECE // 16)])
            nc.tensor.matmul(
                banks[a, q][:],
                weights[k][:, a * P : (a + 1) * P],
                picked,
                start=(k == 0),
                stop=(k == K_BLOCKS - 1),
            )

        def open_bank(a, q):
            banks[a, q] = psum.tile([P, PIECE], F32, name="bank")
            gathered_matmul(0, a, q)

        pooled_blocks = {}

        def close_and_pool(a, q, cuts):
            gathered_matmul(1, a, q)
            if q == 0:
                pooled_blocks[a] = work.tile([P, PIECES * POOLED], F32, name="pooled")
            run = PIECE // cuts
            for c in range(cuts):
                z = work.tile([P, run], F32, name="z")
                nc.scalar.activation(
                    z[:],
                    banks[a, q][:, c * run : (c + 1) * run],
                    mybir.ActivationFunctionType.Gelu_apprx_tanh,
                    bias=bias[:, a : a + 1],
                )
                first = q * POOLED + c * (run // NEIGHBOURS)
                nc.vector.tensor_reduce(
                    pooled_blocks[a][:, first : first + run // NEIGHBOURS],
                    z[:].rearrange("p (v t) -> p v t", t=NEIGHBOURS),
                    axis=mybir.AxisListType.X,
                    op=mybir.AluOpType.max,
                )
            if q == PIECES - 1:
                nc.sync.dma_start(out[a * P : (a + 1) * P, :], pooled_blocks[a][:])

        output_tiles = [(a, q) for a in range(M_BLOCKS) for q in range(PIECES)]
        for a, q in output_tiles[:LEAD]:
            open_bank(a, q)
        for a, q in output_tiles[:LEAD]:
            close_and_pool(a, q, cuts=1)
        for a, q in output_tiles[LEAD:]:
            open_bank(a, q)
            close_and_pool(a, q, cuts=LAST_CUTS)
